import numpy as np
import ml_dtypes


def mxq(x, axis, fmt="e4m3"):
    dtype, down = {"e4m3": (ml_dtypes.float8_e4m3fn, 7), "e5m2": (ml_dtypes.float8_e5m2, 14)}[fmt]
    v = np.moveaxis(np.asarray(x, np.float32).astype(ml_dtypes.bfloat16).astype(np.float64), axis, -1)
    blocks = v.reshape(v.shape[:-1] + (-1, 32))
    amax = np.abs(blocks).max(-1, keepdims=True)
    byte = np.maximum(np.where(amax > 0, np.frexp(amax)[1] - 1 + 127, 0) - down, 1)
    scale = np.exp2(byte - 127.0)
    codes = (blocks / scale).astype(np.float32).astype(dtype).astype(np.float64)
    return np.moveaxis((codes * scale).reshape(v.shape), -1, axis)


WIDE = False


def mx_kscale(k):
    if not WIDE:
        return np.ones(k)
    levels = np.array([10, -10, 5, -5, 0])
    if k % 512:
        return np.exp2(np.random.permutation(np.resize(levels, k // 32))).repeat(32)
    a = np.empty((k // 512, 16))
    for p in range(k // 512):
        a[p, :8] = np.random.permutation(np.resize(levels, 8))
        for g in range(8):
            far = levels[np.abs(levels - a[p, g]) >= 10]
            a[p, g + 8] = far[np.random.randint(len(far))]
    return np.exp2(a.ravel()).repeat(32)


def f64(x):
    return np.asarray(x).astype(np.float64)


def striped(idx):
    return np.tile(idx.reshape(-1, 16).T, (8, 1)).astype(np.uint16)


def unstriped(offs):
    return offs[:16].T.reshape(-1).astype(np.int64)


E2M1 = np.array([0.0, 0.5, 1.0, 1.5, 2.0, 3.0, 4.0, 6.0, -0.0, -0.5, -1.0, -1.5, -2.0, -3.0, -4.0, -6.0])


def pack_weight(w, fmt):
    k, n = w.shape
    w = f64(np.asarray(w, np.float32).astype(ml_dtypes.bfloat16)).reshape(k // 32, 32, n)
    amax = np.abs(w).max(1)
    if fmt == "e4m3":
        byte = np.frexp(amax)[1] - 1 + 127 - 7
    else:
        mant, ex = np.frexp(amax / 6.0)
        byte = np.where(mant > 0.5, ex, ex - 1) + 127
    byte = np.clip(np.where(amax > 0, byte, 1), 1, 254)
    scaled = (w * np.exp2(127.0 - byte)[:, None, :]).reshape(k, n).astype(np.float32)
    by_word = np.ascontiguousarray(scaled.reshape(k // 512, 128, 4, n).transpose(0, 1, 3, 2))
    if fmt == "e4m3":
        words = by_word.astype(ml_dtypes.float8_e4m3fn).view(np.uint8)
    else:
        c = by_word.astype(ml_dtypes.float4_e2m1fn).view(np.uint8) & 0xF
        words = (c[..., 0::2] | (c[..., 1::2] << 4)).reshape(k // 512, 128, 2 * n)
    return np.ascontiguousarray(words), np.ascontiguousarray(byte.astype(np.uint8).reshape(k // 512, 16, n))


def unpack_weight(words, scales, fmt):
    g, _, n = scales.shape
    words = np.ascontiguousarray(words).reshape(g, 128, n, -1)
    if fmt == "e4m3":
        vals = words.view(ml_dtypes.float8_e4m3fn).astype(np.float64)
    else:
        nib = np.empty((g, 128, n, 4), np.uint8)
        nib[..., 0::2] = words & 0xF
        nib[..., 1::2] = words >> 4
        vals = E2M1[nib]
    vals = vals * np.repeat(np.exp2(scales.astype(np.float64) - 127.0), 8, axis=1)[..., None]
    return vals.transpose(0, 1, 3, 2).reshape(g * 512, n)


def relu2(v):
    return np.maximum(v, 0.0) ** 2


K, T, E, C, N = 2048, 768, 9, 256, 128
TOP = 3
K8 = 1024


def by_expert(wq, xq):
    return np.concatenate([wq[e].T @ xq[:, e * C:(e + 1) * C] for e in range(E)], axis=1)


def setup_inputs():
    n = np.random.standard_normal
    s = mx_kscale(K)[:, None]
    deal = np.repeat(np.arange(E), C).reshape(TOP, T)[:, np.random.permutation(T)]
    deal = np.take_along_axis(deal, np.argsort(np.random.rand(TOP, T), axis=0), axis=0)
    for _ in range(8):
        s_, t_ = np.random.permutation(T).reshape(2, -1); r = np.random.randint(TOP, size=T // 2); x, y = deal[r, s_].copy(), deal[r, t_].copy()
        ok = ~((deal[:, s_] == y).any(0) | (deal[:, t_] == x).any(0)); deal[r[ok], s_[ok]] = y[ok]; deal[r[ok], t_[ok]] = x[ok]
    order = np.lexsort((np.random.rand(TOP * T), deal.reshape(-1)))
    slot_token = order % T; pos = np.empty(TOP * T, np.int64); pos[order] = np.arange(TOP * T); pos = pos.reshape(TOP, T)
    g = np.random.uniform(0.5, 1.5, (TOP, T)); g = g / g.sum(0)
    w = n((E, K, N)) / np.sqrt(K) / s[None]
    w8 = [pack_weight(m[:K8], "e4m3") for m in w]
    w4 = [pack_weight(m[K8:], "e2m1") for m in w]
    return {
        "xT": (n((K, T)) * s).astype(np.float32),
        "w8_words": np.stack([m[0] for m in w8]),
        "w8_scales": np.stack([m[1] for m in w8]),
        "w4_words": np.stack([m[0] for m in w4]),
        "w4_scales": np.stack([m[1] for m in w4]),
        "b": (0.3 * n((N, E))).astype(np.float32),
        "gate": np.stack([np.tile(r, (N, 1)) for r in g]).astype(np.float32),
        "offs": striped(slot_token),
        "pos1": striped(pos[0]),
        "pos2": striped(pos[1]),
        "pos3": striped(pos[2]),
    }


def reference(xT, w8_words, w8_scales, w4_words, w4_scales, b, gate, offs, pos1, pos2, pos3):
    idx = unstriped(offs)
    w = np.stack([np.concatenate([unpack_weight(w8_words[e], w8_scales[e], "e4m3"), unpack_weight(w4_words[e], w4_scales[e], "e2m1")]) for e in range(E)])
    xq = mxq(f64(xT)[:, idx], 0, "e4m3")
    y = by_expert(w, xq)
    y = relu2(y + np.repeat(f64(b), C, axis=1))
    return sum(f64(gate[r]) * y[:, unstriped(p)] for r, p in enumerate((pos1, pos2, pos3)))

@@ -1,0 +1,197 @@
+from contextlib import ExitStack
+
+import concourse.mybir as mybir
+
+K, T, E, C, N = 2048, 768, 9, 256, 128
+SLOTS = E * C
+FLOPS = 2 * K * N * SLOTS
+
+F32 = mybir.dt.float32
+BF16 = mybir.dt.bfloat16
+I32 = mybir.dt.int32
+U32 = mybir.dt.uint32
+U16 = mybir.dt.uint16
+U8 = mybir.dt.uint8
+FP8X4 = mybir.dt.float8_e4m3fn_x4
+FP4X4 = mybir.dt.float4_e2m1fn_x4
+ACT = mybir.ActivationFunctionType
+ALU = mybir.AluOpType
+
+P = 128
+PASSES = 4
+PLANE = (4, 8, 0, 12)
+
+
+def tile_moe_tk_lin_relu2_kernel(
+    tc, xT, w8_words, w8_scales, w4_words, w4_scales, b, gate, offs, pos1, pos2, pos3, out
+):
+    nc = tc.nc
+    with ExitStack() as ctx:
+        held = ctx.enter_context(tc.tile_pool(name="held", bufs=1))
+        psum = ctx.enter_context(tc.psum_pool(name="psum", bufs=1))
+
+        offs_t = held.tile([P, SLOTS // 16], U16, name="offs_t")
+        pos_t = [held.tile([P, T // 16], U16, name=f"pos_t{r}") for r in range(3)]
+        x_f = [held.tile([P, 4, T], F32, name=f"x_f{a}") for a in range(PASSES)]
+        x_b = [
+            held.tile([P, T, 4], BF16, name=f"x_b{a}", tag="late" if a == 3 else f"x_b{a}", align_bytes=64)
+            for a in range(PASSES)
+        ]
+        x_w = {}
+        x_s = held.tile([P, T], U8, name="x_s", align_bytes=64)
+        g_w = {a: held.tile([P, SLOTS], U32, name=f"g_w{a}", align_bytes=64) for a in (0, 1, 3)}
+        g_s = held.tile([P, SLOTS], U8, name="g_s", align_bytes=64)
+        m_s = held.tile([P, SLOTS], U8, name="m_s", align_bytes=64)
+        w8_t = held.tile([P, 2 * E, 4 * N], U8, name="w8_t", align_bytes=64)
+        w4_t = held.tile([P, 2 * E, 2 * N], U8, name="w4_t", align_bytes=64)
+        ws_t = held.tile([P, 2, 2 * E, N], U8, name="ws_t", align_bytes=64)
+        b_t = held.tile([P, E], F32, name="b_t")
+        gate_t = held.tile([P, 3, T], F32, name="gate_t")
+        relu_t = held.tile([P, SLOTS], F32, name="relu_t")
+        y_t = held.tile([P, SLOTS], F32, name="y_t")
+        pick = [held.tile([P, T], F32, name=f"pick{r}") for r in range(3)]
+        sum_t = held.tile([P, T], F32, name="sum_t")
+        out_t = held.tile([P, T], F32, name="out_t")
+        warm = held.tile([P, 1], F32, name="warm")
+        bank = [psum.tile([P, 512], F32, name=f"bank{i}") for i in range(8)]
+
+        nc.gpsimd.memset(x_s[:], 0)
+        nc.gpsimd.memset(m_s[:].bitcast(I32), 0)
+        nc.vector.memset(ws_t[:].rearrange("p s g n -> p (s g n)").bitcast(I32), 0)
+        nc.vector.memset(warm[:], 0.0)
+        nc.scalar.activation(warm[:], warm[:], ACT.Square)
+
+        xv = xT.rearrange("(a p j) t -> a p j t", a=PASSES, j=4)
+
+        def load_x(a, c0, c1):
+            nc.sync.dma_start(out=x_f[a][:, :, c0:c1], in_=xv[a, :, :, c0:c1])
+
+        def cast(engine, a, c0, c1):
+            src = x_f[a][:, :, c0:c1].rearrange("p j t -> p t j")
+            if engine == "v":
+                nc.vector.tensor_copy(x_b[a][:, c0:c1, :], src)
+            else:
+                nc.scalar.activation(x_b[a][:, c0:c1, :], src, ACT.Copy)
+
+        def quantise(a, c0, c1):
+            nc.vector.quantize_mx(
+                out=x_w[a][:, c0:c1].bitcast(FP8X4),
+                scales=x_s[PLANE[a] : P, c0:c1],
+                in_=x_b[a][:, c0:c1, :].rearrange("p t j -> p (t j)"),
+            )
+
+        def new_words(a):
+            x_w[a] = held.tile([P, T], U32, name="x_w" if a < 3 else "x_w3", align_bytes=64)
+
+        def gather_words(a, s0, s1):
+            nc.vector.tensor_copy(g_w[a][:, s0:s1], x_w[a][:].indirect(offs_t[:, s0 // 16 : s1 // 16]))
+
+        def gather_scales(s0, s1):
+            nc.vector.tensor_copy(g_s[:, s0:s1], x_s[:].indirect(offs_t[:, s0 // 16 : s1 // 16]))
+
+        head_chunks = ((0, 384), (384, 640), (640, 768))
+        for c0, c1 in head_chunks:
+            load_x(0, c0, c1)
+        nc.sync.dma_start(offs_t[:], offs)
+        for a in (1, 2):
+            for c0 in (0, 384):
+                load_x(a, c0, c0 + 384)
+        for s, scales in enumerate((w8_scales, w4_scales)):
+            for q in range(4):
+                nc.sync.dma_start(
+                    out=ws_t[32 * q : 32 * q + 4, s].bitcast(I32),
+                    in_=scales[:, :, 4 * q : 4 * q + 4, :].rearrange("e a q n -> q (e a) n").bitcast(I32),
+                )
+        for c0 in (0, 384):
+            load_x(3, c0, c0 + 384)
+        nc.sync.dma_start(out=w8_t[:].bitcast(I32), in_=w8_words.rearrange("e a p n r -> p (e a) (n r)").bitcast(I32))
+        nc.sync.dma_start(out=w4_t[:].bitcast(I32), in_=w4_words.rearrange("e a p n -> p (e a) n").bitcast(I32))
+        nc.sync.dma_start(out=b_t[:], in_=b)
+        for t, src in zip(pos_t, (pos1, pos2, pos3)):
+            nc.sync.dma_start(t[:], src)
+        nc.sync.dma_start(out=gate_t[:], in_=gate.rearrange("r p t -> p r t"))
+
+        new_words(0)
+        for c0, c1 in head_chunks:
+            cast("v", 0, c0, c1)
+            for q0 in range(c0, c1, 256):
+                quantise(0, q0, min(q0 + 256, c1))
+        for a in (1, 2, 3):
+            cast("s", a, 0, 384)
+            cast("s", a, 384, 768)
+
+        def quantise_all(a):
+            new_words(a)
+            quantise(a, 0, 512)
+            quantise(a, 512, 768)
+
+        quarter = [(i * 576, (i + 1) * 576) for i in range(4)]
+        for s0, s1 in quarter:
+            gather_words(0, s0, s1)
+        quantise_all(1)
+        for s0, s1 in quarter:
+            gather_words(1, s0, s1)
+        quantise_all(2)
+        quantise_all(3)
+        for s0, s1 in quarter:
+            gather_scales(s0, s1)
+        g_w[2] = held.tile([P, SLOTS], U32, name="g_w2", tag="late", align_bytes=64)
+        for q in range(4):
+            nc.sync.dma_start(
+                out=m_s[32 * q : 32 * q + 4, :].bitcast(I32), in_=g_s[32 * q + 12 : 32 * q + 16, :].bitcast(I32)
+            )
+
+        def acc(g):
+            return bank[g % 8][:, (g // 8) * 128 : (g // 8 + 1) * 128]
+
+        def multiply(g, a):
+            e = g // 2
+            cols = slice(g * 128, (g + 1) * 128)
+            if a < 2:
+                lhsT = w8_t[:, 2 * e + a, :].bitcast(FP8X4)
+            else:
+                lhsT = w4_t[:, 2 * e + a - 2, :].bitcast(FP4X4)
+            nc.tensor.matmul_mx(
+                out=acc(g),
+                lhsT=lhsT,
+                lhsT_scale=ws_t[:, a // 2, 2 * e + a % 2, :],
+                rhs=g_w[a][:, cols].bitcast(FP8X4),
+                rhs_scale=m_s[:, cols] if a == 3 else g_s[PLANE[a] : P, cols],
+                start=(a == 0),
+                stop=(a == PASSES - 1),
+            )
+
+        def activate(g):
+            e = g // 2
+            nc.scalar.activation(relu_t[:, g * 128 : (g + 1) * 128], acc(g), ACT.Relu, bias=b_t[:, e : e + 1])
+
+        def square(s0, s1):
+            nc.scalar.activation(y_t[:, s0:s1], relu_t[:, s0:s1], ACT.Square)
+
+        def open_groups(g0, g1):
+            for g in range(g0, min(g1, SLOTS // 128)):
+                multiply(g, 0)
+                multiply(g, 1)
+
+        open_groups(0, 8)
+        for s0, s1 in ((0, 512), (512, 1024), (1024, 1536), (1536, 2048), (2048, 2304)):
+            gather_words(2, s0, s1)
+            for g in range(s0 // 128, s1 // 128):
+                multiply(g, 2)
+            pieces = ((s0, s1),) if s1 < SLOTS else ((s0, s0 + 128), (s0 + 128, s1))
+            for p0, p1 in pieces:
+                gather_words(3, p0, p1)
+                for g in range(p0 // 128, p1 // 128):
+                    multiply(g, 3)
+                    activate(g)
+                square(p0, p1)
+            open_groups(s0 // 128 + 8, s1 // 128 + 8)
+
+        for r in range(3):
+            nc.vector.tensor_tensor(pick[r][:], y_t[:].indirect(pos_t[r][:]), gate_t[:, r, :], ALU.mult)
+        halves = ((0, 512), (512, 768))
+        for c0, c1 in halves:
+            nc.vector.tensor_tensor(sum_t[:, c0:c1], pick[0][:, c0:c1], pick[1][:, c0:c1], ALU.add)
+        for c0, c1 in halves:
+            nc.vector.tensor_tensor(out_t[:, c0:c1], sum_t[:, c0:c1], pick[2][:, c0:c1], ALU.add)
+            nc.sync.dma_start(out=out[:, c0:c1], in_=out_t[:, c0:c1])

@@ -40,6 +40,7 @@ def tile_moe_tk_lin_relu2_kernel(
         x_w = {}
         x_s = held.tile([P, T], U8, name="x_s", align_bytes=64)
         g_w = {a: held.tile([P, SLOTS], U32, name=f"g_w{a}", align_bytes=64) for a in (0, 1, 3)}
+        g_w2 = [held.tile([P, 1024], U32, name="g_w2a", align_bytes=64)]
         g_s = held.tile([P, SLOTS], U8, name="g_s", align_bytes=64)
         m_s = held.tile([P, SLOTS], U8, name="m_s", align_bytes=64)
         w8_t = held.tile([P, 2 * E, 4 * N], U8, name="w8_t", align_bytes=64)
@@ -83,8 +84,13 @@ def tile_moe_tk_lin_relu2_kernel(
         def new_words(a):
             x_w[a] = held.tile([P, T], U32, name="x_w" if a < 3 else "x_w3", align_bytes=64)
 
+        def words(a, s0, s1):
+            if a != 2:
+                return g_w[a][:, s0:s1]
+            return g_w2[0][:, s0:s1] if s1 <= 1024 else g_w2[1][:, s0 - 1024 : s1 - 1024]
+
         def gather_words(a, s0, s1):
-            nc.vector.tensor_copy(g_w[a][:, s0:s1], x_w[a][:].indirect(offs_t[:, s0 // 16 : s1 // 16]))
+            nc.vector.tensor_copy(words(a, s0, s1), x_w[a][:].indirect(offs_t[:, s0 // 16 : s1 // 16]))
 
         def gather_scales(s0, s1):
             nc.vector.tensor_copy(g_s[:, s0:s1], x_s[:].indirect(offs_t[:, s0 // 16 : s1 // 16]))
@@ -93,17 +99,16 @@ def tile_moe_tk_lin_relu2_kernel(
         for c0, c1 in head_chunks:
             load_x(0, c0, c1)
         nc.sync.dma_start(offs_t[:], offs)
-        for a in (1, 2):
-            for c0 in (0, 384):
-                load_x(a, c0, c0 + 384)
+        for c0 in (0, 384):
+            load_x(1, c0, c0 + 384)
+        load_x(2, 0, T)
+        load_x(3, 0, T)
         for s, scales in enumerate((w8_scales, w4_scales)):
             for q in range(4):
                 nc.sync.dma_start(
                     out=ws_t[32 * q : 32 * q + 4, s].bitcast(I32),
                     in_=scales[:, :, 4 * q : 4 * q + 4, :].rearrange("e a q n -> q (e a) n").bitcast(I32),
                 )
-        for c0 in (0, 384):
-            load_x(3, c0, c0 + 384)
         nc.sync.dma_start(out=w8_t[:].bitcast(I32), in_=w8_words.rearrange("e a p n r -> p (e a) (n r)").bitcast(I32))
         nc.sync.dma_start(out=w4_t[:].bitcast(I32), in_=w4_words.rearrange("e a p n -> p (e a) n").bitcast(I32))
         nc.sync.dma_start(out=b_t[:], in_=b)
@@ -132,10 +137,12 @@ def tile_moe_tk_lin_relu2_kernel(
         for s0, s1 in quarter:
             gather_words(1, s0, s1)
         quantise_all(2)
+        for s0, s1 in ((0, 512), (512, 1024)):
+            gather_words(2, s0, s1)
         quantise_all(3)
         for s0, s1 in quarter:
             gather_scales(s0, s1)
-        g_w[2] = held.tile([P, SLOTS], U32, name="g_w2", tag="late", align_bytes=64)
+        g_w2.append(held.tile([P, SLOTS - 1024], U32, name="g_w2b", tag="late", align_bytes=64))
         for q in range(4):
             nc.sync.dma_start(
                 out=m_s[32 * q : 32 * q + 4, :].bitcast(I32), in_=g_s[32 * q + 12 : 32 * q + 16, :].bitcast(I32)
@@ -155,7 +162,7 @@ def tile_moe_tk_lin_relu2_kernel(
                 out=acc(g),
                 lhsT=lhsT,
                 lhsT_scale=ws_t[:, a // 2, 2 * e + a % 2, :],
-                rhs=g_w[a][:, cols].bitcast(FP8X4),
+                rhs=words(a, cols.start, cols.stop).bitcast(FP8X4),
                 rhs_scale=m_s[:, cols] if a == 3 else g_s[PLANE[a] : P, cols],
                 start=(a == 0),
                 stop=(a == PASSES - 1),
@@ -163,6 +170,11 @@ def tile_moe_tk_lin_relu2_kernel(
 
         def activate(g):
             e = g // 2
+            if g == SLOTS // 128 - 1:
+                nc.vector.tensor_scalar(
+                    relu_t[:, g * 128 : (g + 1) * 128], acc(g), b_t[:, e : e + 1], 0.0, ALU.add, ALU.max
+                )
+                return
             nc.scalar.activation(relu_t[:, g * 128 : (g + 1) * 128], acc(g), ACT.Relu, bias=b_t[:, e : e + 1])
 
         def square(s0, s1):
@@ -175,7 +187,8 @@ def tile_moe_tk_lin_relu2_kernel(
 
         open_groups(0, 8)
         for s0, s1 in ((0, 512), (512, 1024), (1024, 1536), (1536, 2048), (2048, 2304)):
-            gather_words(2, s0, s1)
+            if s0 >= 1024:
+                gather_words(2, s0, s1)
             for g in range(s0 // 128, s1 // 128):
                 multiply(g, 2)
             pieces = ((s0, s1),) if s1 < SLOTS else ((s0, s0 + 128), (s0 + 128, s1))
@@ -184,7 +197,10 @@ def tile_moe_tk_lin_relu2_kernel(
                 for g in range(p0 // 128, p1 // 128):
                     multiply(g, 3)
                     activate(g)
-                square(p0, p1)
+                if p1 < SLOTS:
+                    square(p0, p1)
+                else:
+                    nc.vector.tensor_tensor(y_t[:, p0:p1], relu_t[:, p0:p1], relu_t[:, p0:p1], ALU.mult)
             open_groups(s0 // 128 + 8, s1 // 128 + 8)
 
         for r in range(3):

@@ -82,7 +82,7 @@ def tile_moe_tk_lin_relu2_kernel(
             )
 
         def new_words(a):
-            x_w[a] = held.tile([P, T], U32, name="x_w" if a < 3 else "x_w3", align_bytes=64)
+            x_w[a] = held.tile([P, T], U32, name=f"x_w{a}", align_bytes=64)
 
         def words(a, s0, s1):
             if a != 2:
@@ -95,8 +95,8 @@ def tile_moe_tk_lin_relu2_kernel(
         def gather_scales(s0, s1):
             nc.vector.tensor_copy(g_s[:, s0:s1], x_s[:].indirect(offs_t[:, s0 // 16 : s1 // 16]))
 
-        head_chunks = ((0, 384), (384, 640), (640, 768))
-        for c0, c1 in head_chunks:
+        head_chunks = ((0, 384, 512), (512, 704, 768))
+        for c0, cm, c1 in head_chunks:
             load_x(0, c0, c1)
         nc.sync.dma_start(offs_t[:], offs)
         for c0 in (0, 384):
@@ -117,10 +117,10 @@ def tile_moe_tk_lin_relu2_kernel(
         nc.sync.dma_start(out=gate_t[:], in_=gate.rearrange("r p t -> p r t"))
 
         new_words(0)
-        for c0, c1 in head_chunks:
-            cast("v", 0, c0, c1)
-            for q0 in range(c0, c1, 256):
-                quantise(0, q0, min(q0 + 256, c1))
+        for c0, cm, c1 in head_chunks:
+            cast("s", 0, cm, c1)
+            cast("v", 0, c0, cm)
+            quantise(0, c0, c1)
         for a in (1, 2, 3):
             cast("s", a, 0, 384)
             cast("s", a, 384, 768)
@@ -131,15 +131,14 @@ def tile_moe_tk_lin_relu2_kernel(
             quantise(a, 512, 768)
 
         quarter = [(i * 576, (i + 1) * 576) for i in range(4)]
-        for s0, s1 in quarter:
-            gather_words(0, s0, s1)
-        quantise_all(1)
-        for s0, s1 in quarter:
-            gather_words(1, s0, s1)
-        quantise_all(2)
-        for s0, s1 in ((0, 512), (512, 1024)):
-            gather_words(2, s0, s1)
+        for a in (0, 1):
+            for s0, s1 in quarter[:3]:
+                gather_words(a, s0, s1)
+            quantise_all(a + 1)
+            gather_words(a, *quarter[3])
+        gather_words(2, 0, 512)
         quantise_all(3)
+        gather_words(2, 512, 1024)
         for s0, s1 in quarter:
             gather_scales(s0, s1)
         g_w2.append(held.tile([P, SLOTS - 1024], U32, name="g_w2b", tag="late", align_bytes=64))

@@ -68,11 +68,12 @@ def tile_moe_tk_lin_relu2_kernel(
             nc.sync.dma_start(out=x_f[a][:, :, c0:c1], in_=xv[a, :, :, c0:c1])
 
         def cast(engine, a, c0, c1):
-            src = x_f[a][:, :, c0:c1].rearrange("p j t -> p t j")
+            src = x_f[a][:, :, c0:c1].rearrange("p j (c i) -> p c j i", i=4)
+            dst = x_b[a][:, c0:c1, :].rearrange("p (c i) j -> p c j i", i=4)
             if engine == "v":
-                nc.vector.tensor_copy(x_b[a][:, c0:c1, :], src)
+                nc.vector.tensor_copy(dst, src)
             else:
-                nc.scalar.activation(x_b[a][:, c0:c1, :], src, ACT.Copy)
+                nc.scalar.activation(dst, src, ACT.Copy)
 
         def quantise(a, c0, c1):
             nc.vector.quantize_mx(
@@ -134,19 +135,23 @@ def tile_moe_tk_lin_relu2_kernel(
         for a in (0, 1):
             for s0, s1 in quarter[:3]:
                 gather_words(a, s0, s1)
-            quantise_all(a + 1)
-            gather_words(a, *quarter[3])
+            new_words(a + 1)
+            quantise(a + 1, 0, 512)
+            gather_words(a, 1728, 2016)
+            quantise(a + 1, 512, 768)
+            gather_words(a, 2016, 2304)
         gather_words(2, 0, 512)
         quantise_all(3)
         gather_words(2, 512, 1024)
-        for s0, s1 in quarter:
-            gather_scales(s0, s1)
+        for h0, h1 in ((0, 1152), (1152, 2304)):
+            for s0 in (h0, h0 + 576):
+                gather_scales(s0, s0 + 576)
+            for q in range(4):
+                nc.sync.dma_start(
+                    out=m_s[32 * q : 32 * q + 4, h0:h1].bitcast(I32),
+                    in_=g_s[32 * q + 12 : 32 * q + 16, h0:h1].bitcast(I32),
+                )
         g_w2.append(held.tile([P, SLOTS - 1024], U32, name="g_w2b", tag="late", align_bytes=64))
-        for q in range(4):
-            nc.sync.dma_start(
-                out=m_s[32 * q : 32 * q + 4, :].bitcast(I32), in_=g_s[32 * q + 12 : 32 * q + 16, :].bitcast(I32)
-            )
-
         def acc(g):
             return bank[g % 8][:, (g // 8) * 128 : (g // 8 + 1) * 128]
 
@@ -196,10 +201,10 @@ def tile_moe_tk_lin_relu2_kernel(
                 for g in range(p0 // 128, p1 // 128):
                     multiply(g, 3)
                     activate(g)
-                if p1 < SLOTS:
-                    square(p0, p1)
-                else:
-                    nc.vector.tensor_tensor(y_t[:, p0:p1], relu_t[:, p0:p1], relu_t[:, p0:p1], ALU.mult)
+            if s1 < SLOTS:
+                square(s0, s1)
+            else:
+                nc.vector.tensor_tensor(y_t[:, s0:s1], relu_t[:, s0:s1], relu_t[:, s0:s1], ALU.mult)
             open_groups(s0 // 128 + 8, s1 // 128 + 8)
 
         for r in range(3):

from contextlib import ExitStack

import concourse.mybir as mybir

K, T, E, C, N = 2048, 768, 9, 256, 128
SLOTS = E * C
FLOPS = 2 * K * N * SLOTS

F32 = mybir.dt.float32
BF16 = mybir.dt.bfloat16
I32 = mybir.dt.int32
U32 = mybir.dt.uint32
U16 = mybir.dt.uint16
U8 = mybir.dt.uint8
FP8X4 = mybir.dt.float8_e4m3fn_x4
FP4X4 = mybir.dt.float4_e2m1fn_x4
ACT = mybir.ActivationFunctionType
ALU = mybir.AluOpType

P = 128
PASSES = 4
PLANE = (4, 8, 0, 12)


def tile_moe_tk_lin_relu2_kernel(
    tc, xT, w8_words, w8_scales, w4_words, w4_scales, b, gate, offs, pos1, pos2, pos3, out
):
    nc = tc.nc
    with ExitStack() as ctx:
        held = ctx.enter_context(tc.tile_pool(name="held", bufs=1))
        psum = ctx.enter_context(tc.psum_pool(name="psum", bufs=1))

        offs_t = held.tile([P, SLOTS // 16], U16, name="offs_t")
        pos_t = [held.tile([P, T // 16], U16, name=f"pos_t{r}") for r in range(3)]
        x_f = [held.tile([P, 4, T], F32, name=f"x_f{a}") for a in range(PASSES)]
        x_b = [
            held.tile([P, T, 4], BF16, name=f"x_b{a}", tag="late" if a == 3 else f"x_b{a}", align_bytes=64)
            for a in range(PASSES)
        ]
        x_w = {}
        x_s = held.tile([P, T], U8, name="x_s", align_bytes=64)
        g_w = {a: held.tile([P, SLOTS], U32, name=f"g_w{a}", align_bytes=64) for a in (0, 1, 3)}
        g_w2 = [held.tile([P, 1024], U32, name="g_w2a", align_bytes=64)]
        g_s = held.tile([P, SLOTS], U8, name="g_s", align_bytes=64)
        m_s = held.tile([P, SLOTS], U8, name="m_s", align_bytes=64)
        w8_t = held.tile([P, 2 * E, 4 * N], U8, name="w8_t", align_bytes=64)
        w4_t = held.tile([P, 2 * E, 2 * N], U8, name="w4_t", align_bytes=64)
        ws_t = held.tile([P, 2, 2 * E, N], U8, name="ws_t", align_bytes=64)
        b_t = held.tile([P, E], F32, name="b_t")
        gate_t = held.tile([P, 3, T], F32, name="gate_t")
        relu_t = held.tile([P, SLOTS], F32, name="relu_t")
        y_t = held.tile([P, SLOTS], F32, name="y_t")
        pick = [held.tile([P, T], F32, name=f"pick{r}") for r in range(3)]
        sum_t = held.tile([P, T], F32, name="sum_t")
        out_t = held.tile([P, T], F32, name="out_t")
        warm = held.tile([P, 1], F32, name="warm")
        bank = [psum.tile([P, 512], F32, name=f"bank{i}") for i in range(8)]

        nc.gpsimd.memset(x_s[:], 0)
        nc.gpsimd.memset(m_s[:].bitcast(I32), 0)
        nc.vector.memset(ws_t[:].rearrange("p s g n -> p (s g n)").bitcast(I32), 0)
        nc.vector.memset(warm[:], 0.0)
        nc.scalar.activation(warm[:], warm[:], ACT.Square)

        xv = xT.rearrange("(a p j) t -> a p j t", a=PASSES, j=4)

        def load_x(a, c0, c1):
            nc.sync.dma_start(out=x_f[a][:, :, c0:c1], in_=xv[a, :, :, c0:c1])

        def cast(engine, a, c0, c1):
            src = x_f[a][:, :, c0:c1].rearrange("p j (c i) -> p c j i", i=4)
            dst = x_b[a][:, c0:c1, :].rearrange("p (c i) j -> p c j i", i=4)
            if engine == "v":
                nc.vector.tensor_copy(dst, src)
            else:
                nc.scalar.activation(dst, src, ACT.Copy)

        def quantise(a, c0, c1):
            nc.vector.quantize_mx(
                out=x_w[a][:, c0:c1].bitcast(FP8X4),
                scales=x_s[PLANE[a] : P, c0:c1],
                in_=x_b[a][:, c0:c1, :].rearrange("p t j -> p (t j)"),
            )

        def new_words(a):
            x_w[a] = held.tile([P, T], U32, name=f"x_w{a}", align_bytes=64)

        def words(a, s0, s1):
            if a != 2:
                return g_w[a][:, s0:s1]
            return g_w2[0][:, s0:s1] if s1 <= 1024 else g_w2[1][:, s0 - 1024 : s1 - 1024]

        def gather_words(a, s0, s1):
            nc.vector.tensor_copy(words(a, s0, s1), x_w[a][:].indirect(offs_t[:, s0 // 16 : s1 // 16]))

        def gather_scales(s0, s1):
            nc.vector.tensor_copy(g_s[:, s0:s1], x_s[:].indirect(offs_t[:, s0 // 16 : s1 // 16]))

        head_chunks = ((0, 384, 512), (512, 704, 768))
        for c0, cm, c1 in head_chunks:
            load_x(0, c0, c1)
        nc.sync.dma_start(offs_t[:], offs)
        for c0 in (0, 384):
            load_x(1, c0, c0 + 384)
        load_x(2, 0, T)
        load_x(3, 0, T)
        for s, scales in enumerate((w8_scales, w4_scales)):
            for q in range(4):
                nc.sync.dma_start(
                    out=ws_t[32 * q : 32 * q + 4, s].bitcast(I32),
                    in_=scales[:, :, 4 * q : 4 * q + 4, :].rearrange("e a q n -> q (e a) n").bitcast(I32),
                )
        nc.sync.dma_start(out=w8_t[:].bitcast(I32), in_=w8_words.rearrange("e a p n r -> p (e a) (n r)").bitcast(I32))
        nc.sync.dma_start(out=w4_t[:].bitcast(I32), in_=w4_words.rearrange("e a p n -> p (e a) n").bitcast(I32))
        nc.sync.dma_start(out=b_t[:], in_=b)
        for t, src in zip(pos_t, (pos1, pos2, pos3)):
            nc.sync.dma_start(t[:], src)
        nc.sync.dma_start(out=gate_t[:], in_=gate.rearrange("r p t -> p r t"))

        new_words(0)
        for c0, cm, c1 in head_chunks:
            cast("s", 0, cm, c1)
            cast("v", 0, c0, cm)
            quantise(0, c0, c1)
        for a in (1, 2, 3):
            cast("s", a, 0, 384)
            cast("s", a, 384, 768)

        def quantise_all(a):
            new_words(a)
            quantise(a, 0, 512)
            quantise(a, 512, 768)

        quarter = [(i * 576, (i + 1) * 576) for i in range(4)]
        for a in (0, 1):
            for s0, s1 in quarter[:3]:
                gather_words(a, s0, s1)
            new_words(a + 1)
            quantise(a + 1, 0, 512)
            gather_words(a, 1728, 2016)
            quantise(a + 1, 512, 768)
            gather_words(a, 2016, 2304)
        gather_words(2, 0, 512)
        quantise_all(3)
        gather_words(2, 512, 1024)
        for h0, h1 in ((0, 1152), (1152, 2304)):
            for s0 in (h0, h0 + 576):
                gather_scales(s0, s0 + 576)
            for q in range(4):
                nc.sync.dma_start(
                    out=m_s[32 * q : 32 * q + 4, h0:h1].bitcast(I32),
                    in_=g_s[32 * q + 12 : 32 * q + 16, h0:h1].bitcast(I32),
                )
        g_w2.append(held.tile([P, SLOTS - 1024], U32, name="g_w2b", tag="late", align_bytes=64))
        def acc(g):
            return bank[g % 8][:, (g // 8) * 128 : (g // 8 + 1) * 128]

        def multiply(g, a):
            e = g // 2
            cols = slice(g * 128, (g + 1) * 128)
            if a < 2:
                lhsT = w8_t[:, 2 * e + a, :].bitcast(FP8X4)
            else:
                lhsT = w4_t[:, 2 * e + a - 2, :].bitcast(FP4X4)
            nc.tensor.matmul_mx(
                out=acc(g),
                lhsT=lhsT,
                lhsT_scale=ws_t[:, a // 2, 2 * e + a % 2, :],
                rhs=words(a, cols.start, cols.stop).bitcast(FP8X4),
                rhs_scale=m_s[:, cols] if a == 3 else g_s[PLANE[a] : P, cols],
                start=(a == 0),
                stop=(a == PASSES - 1),
            )

        def activate(g):
            e = g // 2
            if g == SLOTS // 128 - 1:
                nc.vector.tensor_scalar(
                    relu_t[:, g * 128 : (g + 1) * 128], acc(g), b_t[:, e : e + 1], 0.0, ALU.add, ALU.max
                )
                return
            nc.scalar.activation(relu_t[:, g * 128 : (g + 1) * 128], acc(g), ACT.Relu, bias=b_t[:, e : e + 1])

        def square(s0, s1):
            nc.scalar.activation(y_t[:, s0:s1], relu_t[:, s0:s1], ACT.Square)

        def open_groups(g0, g1):
            for g in range(g0, min(g1, SLOTS // 128)):
                multiply(g, 0)
                multiply(g, 1)

        open_groups(0, 8)
        for s0, s1 in ((0, 512), (512, 1024), (1024, 1536), (1536, 2048), (2048, 2304)):
            if s0 >= 1024:
                gather_words(2, s0, s1)
            for g in range(s0 // 128, s1 // 128):
                multiply(g, 2)
            pieces = ((s0, s1),) if s1 < SLOTS else ((s0, s0 + 128), (s0 + 128, s1))
            for p0, p1 in pieces:
                gather_words(3, p0, p1)
                for g in range(p0 // 128, p1 // 128):
                    multiply(g, 3)
                    activate(g)
            if s1 < SLOTS:
                square(s0, s1)
            else:
                nc.vector.tensor_tensor(y_t[:, s0:s1], relu_t[:, s0:s1], relu_t[:, s0:s1], ALU.mult)
            open_groups(s0 // 128 + 8, s1 // 128 + 8)

        for r in range(3):
            nc.vector.tensor_tensor(pick[r][:], y_t[:].indirect(pos_t[r][:]), gate_t[:, r, :], ALU.mult)
        halves = ((0, 512), (512, 768))
        for c0, c1 in halves:
            nc.vector.tensor_tensor(sum_t[:, c0:c1], pick[0][:, c0:c1], pick[1][:, c0:c1], ALU.add)
        for c0, c1 in halves:
            nc.vector.tensor_tensor(out_t[:, c0:c1], sum_t[:, c0:c1], pick[2][:, c0:c1], ALU.add)
            nc.sync.dma_start(out=out[:, c0:c1], in_=out_t[:, c0:c1])
